import numpy as np
import ml_dtypes


def mxq(x, axis, fmt="e4m3"):
    dtype, down = {"e4m3": (ml_dtypes.float8_e4m3fn, 7), "e5m2": (ml_dtypes.float8_e5m2, 14)}[fmt]
    v = np.moveaxis(np.asarray(x, np.float32).astype(ml_dtypes.bfloat16).astype(np.float64), axis, -1)
    blocks = v.reshape(v.shape[:-1] + (-1, 32))
    amax = np.abs(blocks).max(-1, keepdims=True)
    byte = np.maximum(np.where(amax > 0, np.frexp(amax)[1] - 1 + 127, 0) - down, 1)
    scale = np.exp2(byte - 127.0)
    codes = (blocks / scale).astype(np.float32).astype(dtype).astype(np.float64)
    return np.moveaxis((codes * scale).reshape(v.shape), -1, axis)


WIDE = False


def mx_kscale(k):
    if not WIDE:
        return np.ones(k)
    levels = np.array([10, -10, 5, -5, 0])
    if k % 512:
        return np.exp2(np.random.permutation(np.resize(levels, k // 32))).repeat(32)
    a = np.empty((k // 512, 16))
    for p in range(k // 512):
        a[p, :8] = np.random.permutation(np.resize(levels, 8))
        for g in range(8):
            far = levels[np.abs(levels - a[p, g]) >= 10]
            a[p, g + 8] = far[np.random.randint(len(far))]
    return np.exp2(a.ravel()).repeat(32)


def f64(x):
    return np.asarray(x).astype(np.float64)


def striped8(idx):
    return np.asarray(idx).reshape(8, -1, 16).transpose(0, 2, 1).reshape(128, -1).astype(np.uint16)


def unstriped8(offs):
    return offs.reshape(8, 16, -1).transpose(0, 2, 1).reshape(8, -1).astype(np.int64)


def pick8(x, idx, run):
    r = np.arange(len(x))
    return x[r[:, None], idx[r % (8 * run) // run]]


E2M1 = np.array([0.0, 0.5, 1.0, 1.5, 2.0, 3.0, 4.0, 6.0, -0.0, -0.5, -1.0, -1.5, -2.0, -3.0, -4.0, -6.0])


def pack_weight(w, fmt):
    k, n = w.shape
    w = f64(np.asarray(w, np.float32).astype(ml_dtypes.bfloat16)).reshape(k // 32, 32, n)
    amax = np.abs(w).max(1)
    if fmt == "e4m3":
        byte = np.frexp(amax)[1] - 1 + 127 - 7
    else:
        mant, ex = np.frexp(amax / 6.0)
        byte = np.where(mant > 0.5, ex, ex - 1) + 127
    byte = np.clip(np.where(amax > 0, byte, 1), 1, 254)
    scaled = (w * np.exp2(127.0 - byte)[:, None, :]).reshape(k, n).astype(np.float32)
    by_word = np.ascontiguousarray(scaled.reshape(k // 512, 128, 4, n).transpose(0, 1, 3, 2))
    if fmt == "e4m3":
        words = by_word.astype(ml_dtypes.float8_e4m3fn).view(np.uint8)
    else:
        c = by_word.astype(ml_dtypes.float4_e2m1fn).view(np.uint8) & 0xF
        words = (c[..., 0::2] | (c[..., 1::2] << 4)).reshape(k // 512, 128, 2 * n)
    return np.ascontiguousarray(words), np.ascontiguousarray(byte.astype(np.uint8).reshape(k // 512, 16, n))


def unpack_weight(words, scales, fmt):
    g, _, n = scales.shape
    words = np.ascontiguousarray(words).reshape(g, 128, n, -1)
    if fmt == "e4m3":
        vals = words.view(ml_dtypes.float8_e4m3fn).astype(np.float64)
    else:
        nib = np.empty((g, 128, n, 4), np.uint8)
        nib[..., 0::2] = words & 0xF
        nib[..., 1::2] = words >> 4
        vals = E2M1[nib]
    vals = vals * np.repeat(np.exp2(scales.astype(np.float64) - 127.0), 8, axis=1)[..., None]
    return vals.transpose(0, 1, 3, 2).reshape(g * 512, n)


D, T, U, X, I, O, Q = 512, 1024, 1024, 1024, 512, 2048, 128


def setup_inputs():
    n = np.random.standard_normal
    idx = np.stack([np.random.permutation(X)[:I] for _ in range(8)])
    idx2 = np.stack([np.random.permutation(O)[:I] for _ in range(8)])
    idx3 = np.stack([np.random.permutation(O)[:I] for _ in range(8)])
    idx4 = np.stack([np.random.permutation(X)[:I] for _ in range(8)])
    fd = mx_kscale(D)
    cachep = pack_weight(n((D, T)) / fd[:, None], "e2m1")
    draftp = pack_weight(n((D, U)) / fd[:, None], "e4m3")
    archp = pack_weight(n((D, X)) / fd[:, None], "e2m1")
    return {
        "query": (n((D, Q)) * 1.0 / np.sqrt(D) * fd[:, None]).astype(np.float32),
        "cache_words": cachep[0],
        "cache_scales": cachep[1],
        "draft_words": draftp[0],
        "draft_scales": draftp[1],
        "arch_words": archp[0],
        "arch_scales": archp[1],
        "offs": striped8(idx),
        "offs2": striped8(idx2),
        "offs3": striped8(idx3),
        "offs4": striped8(idx4),
    }


def reference(query, cache_words, cache_scales, draft_words, draft_scales, arch_words, arch_scales, offs, offs2, offs3, offs4):
    idx = unstriped8(offs)
    idx2 = unstriped8(offs2)
    idx3 = unstriped8(offs3)
    idx4 = unstriped8(offs4)
    cacheu = unpack_weight(cache_words, cache_scales, "e2m1")
    draftu = unpack_weight(draft_words, draft_scales, "e4m3")
    archu = unpack_weight(arch_words, arch_scales, "e2m1")
    queryq = mxq(f64(query), 0, "e4m3")
    a = queryq.T @ cacheu
    b = queryq.T @ draftu
    c0 = queryq.T @ archu
    ab = np.concatenate([a, b], axis=1)
    f1 = np.zeros((Q, O))
    f1[np.arange(Q)[:, None], idx2[np.arange(Q) % 128 // 16]] = pick8(c0, idx, 16)
    mo = np.maximum(ab, f1)
    f2 = np.zeros((Q, X))
    f2[np.arange(Q)[:, None], idx4[np.arange(Q) % 128 // 16]] = pick8(mo, idx3, 16)
    cc = c0 - f2
    y = pick8(cc, idx, 16)
    return y

@@ -1,0 +1,138 @@
+from contextlib import ExitStack
+
+import concourse.mybir as mybir
+
+D, POOL, PAGE, SLOTS, Q = 512, 1024, 2048, 512, 128
+FLOPS = 2 * D * Q * 3 * POOL
+
+F32 = mybir.dt.float32
+BF16 = mybir.dt.bfloat16
+I32 = mybir.dt.int32
+U32 = mybir.dt.uint32
+U16 = mybir.dt.uint16
+U8 = mybir.dt.uint8
+FP8X4 = mybir.dt.float8_e4m3fn_x4
+FP4X4 = mybir.dt.float4_e2m1fn_x4
+COPY = mybir.ActivationFunctionType.Copy
+MAX = mybir.AluOpType.max
+SUBTRACT = mybir.AluOpType.subtract
+
+P = 128
+PACK = 4
+BANK = 512
+HALF = SLOTS // 2
+LIST_COLS = SLOTS // 16
+ARCH_N = 256
+
+
+def load_scale_rows(queue, plane, scales):
+    for r in range(4):
+        queue.dma_start(out=plane[r:P:32, :].bitcast(I32), in_=scales[0, r:16:4, :].bitcast(I32))
+
+
+def tile_attend_endwrite_three_kernel(
+    tc, query, cache_words, cache_scales, draft_words, draft_scales, arch_words, arch_scales,
+    offs, offs2, offs3, offs4, out,
+):
+    nc = tc.nc
+    with ExitStack() as ctx:
+        lists = ctx.enter_context(tc.tile_pool(name="lists", bufs=1))
+        sb = ctx.enter_context(tc.tile_pool(name="sb", bufs=1))
+        psum = ctx.enter_context(tc.psum_pool(name="psum", bufs=1))
+
+        idx = lists.tile([P, LIST_COLS], U16, name="idx")
+        idx2 = lists.tile([P, LIST_COLS], U16, name="idx2")
+        idx3 = lists.tile([P, LIST_COLS], U16, name="idx3")
+        idx4 = lists.tile([P, LIST_COLS], U16, name="idx4")
+
+        arch_plane = sb.tile([P, POOL], U8, name="arch_plane", align_bytes=64)
+        cache_plane = sb.tile([P, POOL], U8, name="cache_plane", align_bytes=64)
+        draft_plane = sb.tile([P, POOL], U8, name="draft_plane", align_bytes=64)
+        for plane in (arch_plane, cache_plane, draft_plane):
+            nc.vector.memset(plane[:].bitcast(U32), 0)
+        f1 = sb.tile([P, PAGE], F32, name="f1")
+        nc.vector.memset(f1[:], 0.0)
+
+        q_raw = sb.tile([P, PACK, Q], F32, name="q_raw")
+        arch_codes = sb.tile([P, 2 * POOL], U8, name="arch_codes", align_bytes=64)
+        cache_codes = sb.tile([P, 2 * POOL], U8, name="cache_codes", tag="cache_then_f2", align_bytes=64)
+        draft_codes = sb.tile([P, POOL], U32, name="draft_codes", align_bytes=64)
+
+        nc.sync.dma_start(out=q_raw[:], in_=query.rearrange("(p t) q -> p t q", t=PACK))
+        nc.sync.dma_start(out=arch_codes[:].bitcast(I32), in_=arch_words[0].bitcast(I32))
+        load_scale_rows(nc.scalar, arch_plane, arch_scales)
+        nc.sync.dma_start(idx[:], offs)
+        nc.sync.dma_start(idx2[:], offs2)
+        nc.sync.dma_start(out=cache_codes[:].bitcast(I32), in_=cache_words[0].bitcast(I32))
+        load_scale_rows(nc.sync, cache_plane, cache_scales)
+        nc.sync.dma_start(
+            out=draft_codes[:].bitcast(I32),
+            in_=draft_words[0].rearrange("p n t -> p (n t)").bitcast(I32),
+        )
+        load_scale_rows(nc.sync, draft_plane, draft_scales)
+        nc.sync.dma_start(idx3[:], offs3)
+        nc.sync.dma_start(idx4[:], offs4)
+
+        q_bf = sb.tile([P, Q, PACK], BF16, name="q_bf", align_bytes=64)
+        nc.vector.tensor_copy(out=q_bf[:], in_=q_raw[:].rearrange("p t q -> p q t"))
+        q_codes = sb.tile([P, Q], U32, name="q_codes", align_bytes=64)
+        q_plane = sb.tile([P, Q], U8, name="q_plane", align_bytes=64)
+        nc.vector.quantize_mx(
+            out=q_codes[:].bitcast(FP8X4), scales=q_plane[:], in_=q_bf[:].rearrange("p q t -> p (q t)")
+        )
+
+        def scores(bank, codes, plane):
+            nc.tensor.matmul_mx(
+                out=bank[:], lhsT=q_codes[:].bitcast(FP8X4), lhsT_scale=q_plane[:],
+                rhs=codes, rhs_scale=plane, start=True, stop=True,
+            )
+
+        c0 = sb.tile([P, POOL], F32, name="c0")
+        for j in range(POOL // ARCH_N):
+            cols = slice(j * ARCH_N, (j + 1) * ARCH_N)
+            bank = psum.tile([P, ARCH_N], F32, name=f"arch_bank{j}")
+            scores(bank, arch_codes[:, 2 * cols.start : 2 * cols.stop].bitcast(FP4X4), arch_plane[:, cols])
+            if j % 2 == 0:
+                nc.scalar.copy(out=c0[:, cols], in_=bank[:])
+            else:
+                nc.vector.tensor_copy(out=c0[:, cols], in_=bank[:])
+
+        page_banks = []
+        for j in range(POOL // BANK):
+            cols = slice(j * BANK, (j + 1) * BANK)
+            bank = psum.tile([P, BANK], F32, name=f"cache_bank{j}")
+            scores(bank, cache_codes[:, 2 * cols.start : 2 * cols.stop].bitcast(FP4X4), cache_plane[:, cols])
+            page_banks.append(bank)
+        for j in range(POOL // BANK):
+            cols = slice(j * BANK, (j + 1) * BANK)
+            bank = psum.tile([P, BANK], F32, name=f"draft_bank{j}")
+            scores(bank, draft_codes[:, cols].bitcast(FP8X4), draft_plane[:, cols])
+            page_banks.append(bank)
+
+        halves = [slice(h * LIST_COLS // 2, (h + 1) * LIST_COLS // 2) for h in range(2)]
+        for h in range(2):
+            picked = sb.tile([P, HALF], F32, name=f"picked{h}")
+            nc.vector.tensor_copy(picked[:], c0[:].indirect(idx[:, halves[h]]))
+            nc.scalar.activation(f1[:].indirect(idx2[:, halves[h]]), picked[:], COPY)
+
+        f2 = sb.tile([P, POOL], F32, name="f2", tag="cache_then_f2", align_bytes=64)
+        nc.vector.memset(f2[:], 0.0)
+
+        mo = sb.tile([P, PAGE], F32, name="mo")
+        for j, bank in enumerate(page_banks):
+            cols = slice(j * BANK, (j + 1) * BANK)
+            nc.vector.tensor_tensor(mo[:, cols], bank[:], f1[:, cols], MAX)
+
+        taken = sb.tile([P, SLOTS], F32, name="taken")
+        nc.vector.tensor_copy(taken[:], mo[:].indirect(idx3[:]))
+        nc.scalar.activation(f2[:].indirect(idx4[:]), taken[:], COPY)
+
+        cc = sb.tile([P, POOL], F32, name="cc")
+        nc.vector.tensor_tensor(cc[:], c0[:], f2[:], SUBTRACT)
+
+        left0 = sb.tile([P, HALF], F32, name="left0")
+        left1 = sb.tile([P, HALF], F32, name="left1")
+        nc.vector.tensor_copy(left0[:], cc[:].indirect(idx[:, halves[0]]))
+        nc.sync.dma_start(out=out[:, :HALF], in_=left0[:])
+        nc.scalar.activation(left1[:], cc[:].indirect(idx[:, halves[1]]), COPY)
+        nc.scalar.dma_start(out=out[:, HALF:], in_=left1[:])

@@ -46,23 +46,23 @@ def tile_attend_endwrite_three_kernel(
         idx4 = lists.tile([P, LIST_COLS], U16, name="idx4")
 
         arch_plane = sb.tile([P, POOL], U8, name="arch_plane", align_bytes=64)
-        cache_plane = sb.tile([P, POOL], U8, name="cache_plane", align_bytes=64)
-        draft_plane = sb.tile([P, POOL], U8, name="draft_plane", align_bytes=64)
-        for plane in (arch_plane, cache_plane, draft_plane):
-            nc.vector.memset(plane[:].bitcast(U32), 0)
+        nc.vector.memset(arch_plane[:].bitcast(U32), 0)
+        page_plane = sb.tile([P, PAGE], U8, name="page_plane", align_bytes=64)
+        nc.vector.memset(page_plane[:].bitcast(U32), 0)
         f1 = sb.tile([P, PAGE], F32, name="f1")
         nc.vector.memset(f1[:], 0.0)
 
         q_raw = sb.tile([P, PACK, Q], F32, name="q_raw")
         arch_codes = sb.tile([P, 2 * POOL], U8, name="arch_codes", align_bytes=64)
-        cache_codes = sb.tile([P, 2 * POOL], U8, name="cache_codes", tag="cache_then_f2", align_bytes=64)
-        draft_codes = sb.tile([P, POOL], U32, name="draft_codes", align_bytes=64)
 
         nc.sync.dma_start(out=q_raw[:], in_=query.rearrange("(p t) q -> p t q", t=PACK))
         nc.sync.dma_start(out=arch_codes[:].bitcast(I32), in_=arch_words[0].bitcast(I32))
-        load_scale_rows(nc.scalar, arch_plane, arch_scales)
+        load_scale_rows(nc.sync, arch_plane, arch_scales)
         nc.sync.dma_start(idx[:], offs)
         nc.sync.dma_start(idx2[:], offs2)
+        cache_plane, draft_plane = page_plane[:, :POOL], page_plane[:, POOL:]
+        cache_codes = sb.tile([P, 2 * POOL], U8, name="cache_codes", tag="cache_then_f2", align_bytes=64)
+        draft_codes = sb.tile([P, POOL], U32, name="draft_codes", align_bytes=64)
         nc.sync.dma_start(out=cache_codes[:].bitcast(I32), in_=cache_words[0].bitcast(I32))
         load_scale_rows(nc.sync, cache_plane, cache_scales)
         nc.sync.dma_start(
@@ -74,7 +74,10 @@ def tile_attend_endwrite_three_kernel(
         nc.sync.dma_start(idx4[:], offs4)
 
         q_bf = sb.tile([P, Q, PACK], BF16, name="q_bf", align_bytes=64)
-        nc.vector.tensor_copy(out=q_bf[:], in_=q_raw[:].rearrange("p t q -> p q t"))
+        nc.vector.tensor_copy(
+            out=q_bf[:].rearrange("p (c i) t -> p c t i", i=4),
+            in_=q_raw[:].rearrange("p t (c i) -> p c t i", i=4),
+        )
         q_codes = sb.tile([P, Q], U32, name="q_codes", align_bytes=64)
         q_plane = sb.tile([P, Q], U8, name="q_plane", align_bytes=64)
         nc.vector.quantize_mx(
@@ -110,13 +113,13 @@ def tile_attend_endwrite_three_kernel(
             page_banks.append(bank)
 
         halves = [slice(h * LIST_COLS // 2, (h + 1) * LIST_COLS // 2) for h in range(2)]
-        for h in range(2):
-            picked = sb.tile([P, HALF], F32, name=f"picked{h}")
-            nc.vector.tensor_copy(picked[:], c0[:].indirect(idx[:, halves[h]]))
-            nc.scalar.activation(f1[:].indirect(idx2[:, halves[h]]), picked[:], COPY)
+        picked = sb.tile([P, SLOTS], F32, name="picked")
+        nc.vector.tensor_copy(picked[:, :HALF], c0[:].indirect(idx[:, halves[0]]))
+        nc.scalar.activation(picked[:, HALF:], c0[:].indirect(idx[:, halves[1]]), COPY)
+        nc.scalar.activation(f1[:].indirect(idx2[:]), picked[:], COPY)
 
         f2 = sb.tile([P, POOL], F32, name="f2", tag="cache_then_f2", align_bytes=64)
-        nc.vector.memset(f2[:], 0.0)
+        nc.gpsimd.memset(f2[:], 0.0)
 
         mo = sb.tile([P, PAGE], F32, name="mo")
         for j, bank in enumerate(page_banks):

@@ -47,20 +47,21 @@ def tile_attend_endwrite_three_kernel(
 
         arch_plane = sb.tile([P, POOL], U8, name="arch_plane", align_bytes=64)
         nc.vector.memset(arch_plane[:].bitcast(U32), 0)
-        page_plane = sb.tile([P, PAGE], U8, name="page_plane", align_bytes=64)
-        nc.vector.memset(page_plane[:].bitcast(U32), 0)
+        cache_plane = sb.tile([P, POOL], U8, name="cache_plane", align_bytes=64)
+        nc.vector.memset(cache_plane[:].bitcast(U32), 0)
+        draft_plane = sb.tile([P, POOL], U8, name="draft_plane", align_bytes=64)
+        nc.vector.memset(draft_plane[:].bitcast(U32), 0)
         f1 = sb.tile([P, PAGE], F32, name="f1")
-        nc.vector.memset(f1[:], 0.0)
+        nc.vector.memset(f1[:].bitcast(U32), 0)
 
         q_raw = sb.tile([P, PACK, Q], F32, name="q_raw")
         arch_codes = sb.tile([P, 2 * POOL], U8, name="arch_codes", align_bytes=64)
 
         nc.sync.dma_start(out=q_raw[:], in_=query.rearrange("(p t) q -> p t q", t=PACK))
         nc.sync.dma_start(out=arch_codes[:].bitcast(I32), in_=arch_words[0].bitcast(I32))
-        load_scale_rows(nc.sync, arch_plane, arch_scales)
+        load_scale_rows(nc.scalar, arch_plane, arch_scales)
         nc.sync.dma_start(idx[:], offs)
         nc.sync.dma_start(idx2[:], offs2)
-        cache_plane, draft_plane = page_plane[:, :POOL], page_plane[:, POOL:]
         cache_codes = sb.tile([P, 2 * POOL], U8, name="cache_codes", tag="cache_then_f2", align_bytes=64)
         draft_codes = sb.tile([P, POOL], U32, name="draft_codes", align_bytes=64)
         nc.sync.dma_start(out=cache_codes[:].bitcast(I32), in_=cache_words[0].bitcast(I32))
@@ -73,16 +74,17 @@ def tile_attend_endwrite_three_kernel(
         nc.sync.dma_start(idx3[:], offs3)
         nc.sync.dma_start(idx4[:], offs4)
 
-        q_bf = sb.tile([P, Q, PACK], BF16, name="q_bf", align_bytes=64)
-        nc.vector.tensor_copy(
-            out=q_bf[:].rearrange("p (c i) t -> p c t i", i=4),
-            in_=q_raw[:].rearrange("p t (c i) -> p c t i", i=4),
-        )
         q_codes = sb.tile([P, Q], U32, name="q_codes", align_bytes=64)
         q_plane = sb.tile([P, Q], U8, name="q_plane", align_bytes=64)
-        nc.vector.quantize_mx(
-            out=q_codes[:].bitcast(FP8X4), scales=q_plane[:], in_=q_bf[:].rearrange("p q t -> p (q t)")
-        )
+        q_halves = [slice(h * Q // 2, (h + 1) * Q // 2) for h in range(2)]
+        q_bf = [sb.tile([P, Q // 2, PACK], BF16, name=f"q_bf{h}", align_bytes=64) for h in range(2)]
+        for h, rows in enumerate(q_halves):
+            nc.vector.tensor_copy(out=q_bf[h][:], in_=q_raw[:, :, rows].rearrange("p t q -> p q t"))
+        for h, rows in enumerate(q_halves):
+            nc.vector.quantize_mx(
+                out=q_codes[:, rows].bitcast(FP8X4), scales=q_plane[:, rows],
+                in_=q_bf[h][:].rearrange("p q t -> p (q t)"),
+            )
 
         def scores(bank, codes, plane):
             nc.tensor.matmul_mx(
@@ -91,10 +93,13 @@ def tile_attend_endwrite_three_kernel(
             )
 
         c0 = sb.tile([P, POOL], F32, name="c0")
-        for j in range(POOL // ARCH_N):
-            cols = slice(j * ARCH_N, (j + 1) * ARCH_N)
-            bank = psum.tile([P, ARCH_N], F32, name=f"arch_bank{j}")
+        arch_banks = []
+        arch_edges = [0, 256, 512, 768, 896, 1024]
+        for j in range(len(arch_edges) - 1):
+            cols = slice(arch_edges[j], arch_edges[j + 1])
+            bank = psum.tile([P, cols.stop - cols.start], F32, name=f"arch_bank{j}", tag=f"bank{j}")
             scores(bank, arch_codes[:, 2 * cols.start : 2 * cols.stop].bitcast(FP4X4), arch_plane[:, cols])
+            arch_banks.append(bank)
             if j % 2 == 0:
                 nc.scalar.copy(out=c0[:, cols], in_=bank[:])
             else:
@@ -103,12 +108,12 @@ def tile_attend_endwrite_three_kernel(
         page_banks = []
         for j in range(POOL // BANK):
             cols = slice(j * BANK, (j + 1) * BANK)
-            bank = psum.tile([P, BANK], F32, name=f"cache_bank{j}")
+            bank = psum.tile([P, BANK], F32, name=f"cache_bank{j}", tag=f"bank{5 + j}")
             scores(bank, cache_codes[:, 2 * cols.start : 2 * cols.stop].bitcast(FP4X4), cache_plane[:, cols])
             page_banks.append(bank)
         for j in range(POOL // BANK):
             cols = slice(j * BANK, (j + 1) * BANK)
-            bank = psum.tile([P, BANK], F32, name=f"draft_bank{j}")
+            bank = psum.tile([P, BANK], F32, name=f"draft_bank{j}", tag=f"bank{(7, 3)[j]}")
             scores(bank, draft_codes[:, cols].bitcast(FP8X4), draft_plane[:, cols])
             page_banks.append(bank)
 
@@ -131,7 +136,11 @@ def tile_attend_endwrite_three_kernel(
         nc.scalar.activation(f2[:].indirect(idx4[:]), taken[:], COPY)
 
         cc = sb.tile([P, POOL], F32, name="cc")
-        nc.vector.tensor_tensor(cc[:], c0[:], f2[:], SUBTRACT)
+        for j, bank in enumerate(arch_banks[:3]):
+            cols = slice(arch_edges[j], arch_edges[j + 1])
+            nc.vector.tensor_tensor(cc[:, cols], bank[:], f2[:, cols], SUBTRACT)
+        rest = slice(arch_edges[3], POOL)
+        nc.gpsimd.tensor_tensor(cc[:, rest], c0[:, rest], f2[:, rest], SUBTRACT)
 
         left0 = sb.tile([P, HALF], F32, name="left0")
         left1 = sb.tile([P, HALF], F32, name="left1")

from contextlib import ExitStack

import concourse.mybir as mybir

D, POOL, PAGE, SLOTS, Q = 512, 1024, 2048, 512, 128
FLOPS = 2 * D * Q * 3 * POOL

F32 = mybir.dt.float32
BF16 = mybir.dt.bfloat16
I32 = mybir.dt.int32
U32 = mybir.dt.uint32
U16 = mybir.dt.uint16
U8 = mybir.dt.uint8
FP8X4 = mybir.dt.float8_e4m3fn_x4
FP4X4 = mybir.dt.float4_e2m1fn_x4
COPY = mybir.ActivationFunctionType.Copy
MAX = mybir.AluOpType.max
SUBTRACT = mybir.AluOpType.subtract

P = 128
PACK = 4
BANK = 512
HALF = SLOTS // 2
LIST_COLS = SLOTS // 16
ARCH_N = 256


def load_scale_rows(queue, plane, scales):
    for r in range(4):
        queue.dma_start(out=plane[r:P:32, :].bitcast(I32), in_=scales[0, r:16:4, :].bitcast(I32))


def tile_attend_endwrite_three_kernel(
    tc, query, cache_words, cache_scales, draft_words, draft_scales, arch_words, arch_scales,
    offs, offs2, offs3, offs4, out,
):
    nc = tc.nc
    with ExitStack() as ctx:
        lists = ctx.enter_context(tc.tile_pool(name="lists", bufs=1))
        sb = ctx.enter_context(tc.tile_pool(name="sb", bufs=1))
        psum = ctx.enter_context(tc.psum_pool(name="psum", bufs=1))

        idx = lists.tile([P, LIST_COLS], U16, name="idx")
        idx2 = lists.tile([P, LIST_COLS], U16, name="idx2")
        idx3 = lists.tile([P, LIST_COLS], U16, name="idx3")
        idx4 = lists.tile([P, LIST_COLS], U16, name="idx4")

        arch_plane = sb.tile([P, POOL], U8, name="arch_plane", align_bytes=64)
        nc.vector.memset(arch_plane[:].bitcast(U32), 0)
        cache_plane = sb.tile([P, POOL], U8, name="cache_plane", align_bytes=64)
        nc.vector.memset(cache_plane[:].bitcast(U32), 0)
        draft_plane = sb.tile([P, POOL], U8, name="draft_plane", align_bytes=64)
        nc.vector.memset(draft_plane[:].bitcast(U32), 0)
        f1 = sb.tile([P, PAGE], F32, name="f1")
        nc.vector.memset(f1[:].bitcast(U32), 0)

        q_raw = sb.tile([P, PACK, Q], F32, name="q_raw")
        arch_codes = sb.tile([P, 2 * POOL], U8, name="arch_codes", align_bytes=64)

        nc.sync.dma_start(out=q_raw[:], in_=query.rearrange("(p t) q -> p t q", t=PACK))
        nc.sync.dma_start(out=arch_codes[:].bitcast(I32), in_=arch_words[0].bitcast(I32))
        load_scale_rows(nc.scalar, arch_plane, arch_scales)
        nc.sync.dma_start(idx[:], offs)
        nc.sync.dma_start(idx2[:], offs2)
        cache_codes = sb.tile([P, 2 * POOL], U8, name="cache_codes", tag="cache_then_f2", align_bytes=64)
        draft_codes = sb.tile([P, POOL], U32, name="draft_codes", align_bytes=64)
        nc.sync.dma_start(out=cache_codes[:].bitcast(I32), in_=cache_words[0].bitcast(I32))
        load_scale_rows(nc.sync, cache_plane, cache_scales)
        nc.sync.dma_start(
            out=draft_codes[:].bitcast(I32),
            in_=draft_words[0].rearrange("p n t -> p (n t)").bitcast(I32),
        )
        load_scale_rows(nc.sync, draft_plane, draft_scales)
        nc.sync.dma_start(idx3[:], offs3)
        nc.sync.dma_start(idx4[:], offs4)

        q_codes = sb.tile([P, Q], U32, name="q_codes", align_bytes=64)
        q_plane = sb.tile([P, Q], U8, name="q_plane", align_bytes=64)
        q_halves = [slice(h * Q // 2, (h + 1) * Q // 2) for h in range(2)]
        q_bf = [sb.tile([P, Q // 2, PACK], BF16, name=f"q_bf{h}", align_bytes=64) for h in range(2)]
        for h, rows in enumerate(q_halves):
            nc.vector.tensor_copy(out=q_bf[h][:], in_=q_raw[:, :, rows].rearrange("p t q -> p q t"))
        for h, rows in enumerate(q_halves):
            nc.vector.quantize_mx(
                out=q_codes[:, rows].bitcast(FP8X4), scales=q_plane[:, rows],
                in_=q_bf[h][:].rearrange("p q t -> p (q t)"),
            )

        def scores(bank, codes, plane):
            nc.tensor.matmul_mx(
                out=bank[:], lhsT=q_codes[:].bitcast(FP8X4), lhsT_scale=q_plane[:],
                rhs=codes, rhs_scale=plane, start=True, stop=True,
            )

        c0 = sb.tile([P, POOL], F32, name="c0")
        arch_banks = []
        arch_edges = [0, 256, 512, 768, 896, 1024]
        for j in range(len(arch_edges) - 1):
            cols = slice(arch_edges[j], arch_edges[j + 1])
            bank = psum.tile([P, cols.stop - cols.start], F32, name=f"arch_bank{j}", tag=f"bank{j}")
            scores(bank, arch_codes[:, 2 * cols.start : 2 * cols.stop].bitcast(FP4X4), arch_plane[:, cols])
            arch_banks.append(bank)
            if j % 2 == 0:
                nc.scalar.copy(out=c0[:, cols], in_=bank[:])
            else:
                nc.vector.tensor_copy(out=c0[:, cols], in_=bank[:])

        page_banks = []
        for j in range(POOL // BANK):
            cols = slice(j * BANK, (j + 1) * BANK)
            bank = psum.tile([P, BANK], F32, name=f"cache_bank{j}", tag=f"bank{5 + j}")
            scores(bank, cache_codes[:, 2 * cols.start : 2 * cols.stop].bitcast(FP4X4), cache_plane[:, cols])
            page_banks.append(bank)
        for j in range(POOL // BANK):
            cols = slice(j * BANK, (j + 1) * BANK)
            bank = psum.tile([P, BANK], F32, name=f"draft_bank{j}", tag=f"bank{(7, 3)[j]}")
            scores(bank, draft_codes[:, cols].bitcast(FP8X4), draft_plane[:, cols])
            page_banks.append(bank)

        halves = [slice(h * LIST_COLS // 2, (h + 1) * LIST_COLS // 2) for h in range(2)]
        picked = sb.tile([P, SLOTS], F32, name="picked")
        nc.vector.tensor_copy(picked[:, :HALF], c0[:].indirect(idx[:, halves[0]]))
        nc.scalar.activation(picked[:, HALF:], c0[:].indirect(idx[:, halves[1]]), COPY)
        nc.scalar.activation(f1[:].indirect(idx2[:]), picked[:], COPY)

        f2 = sb.tile([P, POOL], F32, name="f2", tag="cache_then_f2", align_bytes=64)
        nc.gpsimd.memset(f2[:], 0.0)

        mo = sb.tile([P, PAGE], F32, name="mo")
        for j, bank in enumerate(page_banks):
            cols = slice(j * BANK, (j + 1) * BANK)
            nc.vector.tensor_tensor(mo[:, cols], bank[:], f1[:, cols], MAX)

        taken = sb.tile([P, SLOTS], F32, name="taken")
        nc.vector.tensor_copy(taken[:], mo[:].indirect(idx3[:]))
        nc.scalar.activation(f2[:].indirect(idx4[:]), taken[:], COPY)

        cc = sb.tile([P, POOL], F32, name="cc")
        for j, bank in enumerate(arch_banks[:3]):
            cols = slice(arch_edges[j], arch_edges[j + 1])
            nc.vector.tensor_tensor(cc[:, cols], bank[:], f2[:, cols], SUBTRACT)
        rest = slice(arch_edges[3], POOL)
        nc.gpsimd.tensor_tensor(cc[:, rest], c0[:, rest], f2[:, rest], SUBTRACT)

        left0 = sb.tile([P, HALF], F32, name="left0")
        left1 = sb.tile([P, HALF], F32, name="left1")
        nc.vector.tensor_copy(left0[:], cc[:].indirect(idx[:, halves[0]]))
        nc.sync.dma_start(out=out[:, :HALF], in_=left0[:])
        nc.scalar.activation(left1[:], cc[:].indirect(idx[:, halves[1]]), COPY)
        nc.scalar.dma_start(out=out[:, HALF:], in_=left1[:])
